import numpy as np
import ml_dtypes


def mxq(x, axis, fmt="e4m3"):
    dtype, down = {"e4m3": (ml_dtypes.float8_e4m3fn, 7), "e5m2": (ml_dtypes.float8_e5m2, 14)}[fmt]
    v = np.moveaxis(np.asarray(x, np.float32).astype(ml_dtypes.bfloat16).astype(np.float64), axis, -1)
    blocks = v.reshape(v.shape[:-1] + (-1, 32))
    amax = np.abs(blocks).max(-1, keepdims=True)
    byte = np.maximum(np.where(amax > 0, np.frexp(amax)[1] - 1 + 127, 0) - down, 1)
    scale = np.exp2(byte - 127.0)
    codes = (blocks / scale).astype(np.float32).astype(dtype).astype(np.float64)
    return np.moveaxis((codes * scale).reshape(v.shape), -1, axis)


WIDE = False


def mx_kscale(k):
    if not WIDE:
        return np.ones(k)
    levels = np.array([10, -10, 5, -5, 0])
    if k % 512:
        return np.exp2(np.random.permutation(np.resize(levels, k // 32))).repeat(32)
    a = np.empty((k // 512, 16))
    for p in range(k // 512):
        a[p, :8] = np.random.permutation(np.resize(levels, 8))
        for g in range(8):
            far = levels[np.abs(levels - a[p, g]) >= 10]
            a[p, g + 8] = far[np.random.randint(len(far))]
    return np.exp2(a.ravel()).repeat(32)


def f64(x):
    return np.asarray(x).astype(np.float64)


def striped(idx):
    return np.tile(idx.reshape(-1, 16).T, (8, 1)).astype(np.uint16)


def unstriped(offs):
    return offs[:16].T.reshape(-1).astype(np.int64)


def striped8(idx):
    return np.concatenate([x.reshape(-1, 16).T for x in idx]).astype(np.uint16)


def runs(offs, k):
    lists = np.stack([offs[16 * r : 16 * r + 16].T.reshape(-1) for r in range(8)]).astype(np.int64)
    return lists[np.arange(k) % 512 // 64]


def pack_weight(w):
    k, n = w.shape
    w = f64(np.asarray(w, np.float32).astype(ml_dtypes.bfloat16)).reshape(k // 32, 32, n)
    amax = np.abs(w).max(1)
    byte = np.clip(np.where(amax > 0, np.frexp(amax)[1] - 1 + 127 - 7, 1), 1, 254)
    scaled = (w * np.exp2(127.0 - byte)[:, None, :]).reshape(k, n).astype(np.float32)
    words = np.ascontiguousarray(scaled.reshape(k // 512, 128, 4, n).transpose(0, 1, 3, 2)).astype(ml_dtypes.float8_e4m3fn).view(np.uint8)
    return words, np.ascontiguousarray(byte.astype(np.uint8).reshape(k // 512, 16, n))


def unpack_weight(words, scales):
    g, p, n, _ = words.shape
    vals = np.ascontiguousarray(words).view(ml_dtypes.float8_e4m3fn).astype(np.float64) * np.repeat(np.exp2(scales.astype(np.float64) - 127.0), 8, axis=1)[..., None]
    return vals.transpose(0, 1, 3, 2).reshape(g * 512, n)


K, T, S, N, H = 512, 2048, 512, 512, 512
P = 2 ** 7


def setup_inputs():
    n = np.random.standard_normal
    s = mx_kscale(K)[:, None]
    u = mx_kscale(H)
    packed_xT = pack_weight(n((K, T)) * s)
    return {
        "x_words": packed_xT[0],
        "x_scales": packed_xT[1],
        "w1": (n((K, H)) / np.sqrt(K) / s).astype(np.float32),
        "seed": n((H, S)).astype(np.float32),
        "kn": np.tile(np.random.uniform(0.0, 1.0, S), (P, 1)).astype(np.float32),
        "gn": (np.random.uniform(0.5, 1.5, (H, 1)) * u[:, None]).astype(np.float32),
        "w2": (n((H, H)) / np.sqrt(H) / u[:, None]).astype(np.float32),
        "res": n((N, S)).astype(np.float32),
        "w3": (n((H, N)) / np.sqrt(H) / u[:, None]).astype(np.float32),
        "offs": striped(np.random.permutation(T)[:S]),
        "e1": striped8(np.stack([np.random.permutation(S) for _ in range(8)])),
        "e2": striped8(np.stack([np.random.permutation(S) for _ in range(8)])),
        "mv": striped8(np.stack([np.random.permutation(S) for _ in range(8)])),
    }


def reference(x_words, x_scales, w1, seed, kn, gn, w2, res, w3, offs, e1, e2, mv):
    xq = unpack_weight(x_words, x_scales)[:, unstriped(offs)]
    y = mxq(f64(w1), 0, "e4m3").T @ xq
    v1 = 0.75 * (y[np.arange(H)[:, None], runs(e1, H)] + y[np.arange(H)[:, None], runs(e2, H)])
    z = f64(gn) * (v1 + f64(kn)[:1] * (f64(seed) - v1))
    h = np.tanh(mxq(f64(w2), 0, "e4m3").T @ mxq(z, 0, "e4m3"))
    z2 = f64(gn) * (h[np.arange(H)[:, None], runs(mv, H)])
    return f64(res) + (mxq(f64(w3), 0, "e4m3").T @ mxq(z2, 0, "e4m3"))

@@ -1,0 +1,236 @@
+from contextlib import ExitStack
+
+import concourse.mybir as mybir
+
+F32 = mybir.dt.float32
+BF16 = mybir.dt.bfloat16
+I32 = mybir.dt.int32
+U32 = mybir.dt.uint32
+U16 = mybir.dt.uint16
+U8 = mybir.dt.uint8
+FP8X4 = mybir.dt.float8_e4m3fn_x4
+ALU = mybir.AluOpType
+ACT = mybir.ActivationFunctionType
+
+P = 128
+PACK = 4
+T = 2048
+S = 512
+D = 512
+HALF = S // 2
+CHUNKS = ((0, 256), (256, 128), (384, 128))
+W1_VECTOR_SHARE = 80
+
+FLOPS = 3 * 2 * D * D * S
+
+
+def tile_picked_clampprop_none_p_kernel(
+    tc, x_words, x_scales, w1, seed, kn, gn, w2, res, w3, offs, e1, e2, mv, out
+):
+    nc = tc.nc
+    with ExitStack() as ctx:
+        keep = ctx.enter_context(tc.tile_pool(name="keep", bufs=1))
+        psum = ctx.enter_context(tc.psum_pool(name="psum", bufs=8))
+
+        def sb(name, shape, dtype, tag=None):
+            return keep.tile(shape, dtype, name=name, tag=tag or name, align_bytes=64)
+
+        def bank(name, shape):
+            return psum.tile(shape, F32, name=name, tag="bank")
+
+        def rows_dealt(dram):
+            return dram.rearrange("(p t) c -> p t c", t=PACK)
+
+        def load_list(name, dram):
+            tile = keep.tile([P, S // 16], U16, name=name)
+            nc.sync.dma_start(tile[:], dram)
+            return tile
+
+        def load_rows(name, dram, tag):
+            tile = sb(name, [P, PACK, D], F32, tag)
+            nc.sync.dma_start(tile[:], rows_dealt(dram))
+            return tile
+
+        x_scale_table = sb("x_scale_table", [P, T], U8, "small")
+        nc.gpsimd.memset(x_scale_table[:, 0 : T // 2].bitcast(I32), 0)
+        nc.vector.memset(x_scale_table[:, T // 2 : T].bitcast(I32), 0)
+        for q in range(4):
+            nc.scalar.dma_start(
+                x_scale_table[32 * q : 32 * q + 4, :].bitcast(I32),
+                x_scales[0, 4 * q : 4 * q + 4, :].bitcast(I32),
+            )
+        offs_sb = load_list("offs_sb", offs)
+        e1_sb = load_list("e1_sb", e1)
+        w1_raw = load_rows("w1_raw", w1, "big0")
+        x_word_table = sb("x_word_table", [P, T], U32, "big1")
+        nc.sync.dma_start(
+            x_word_table[:].bitcast(I32), x_words[0].rearrange("p n t -> p (n t)").bitcast(I32)
+        )
+        e2_sb = load_list("e2_sb", e2)
+        mv_sb = load_list("mv_sb", mv)
+
+        def deal_views(grouped, raw, m0, m1):
+            dst = grouped[:].rearrange("p (t m j) -> p m j t", t=PACK, j=PACK)[:, m0:m1]
+            src = raw[:].rearrange("p j (m t) -> p m j t", t=PACK)[:, m0:m1]
+            return dst, src
+
+        def quantized(name, grouped, width):
+            codes = sb(name + "_codes", [P, width], U32)
+            scales = sb(name + "_scales", [P, width], U8)
+            nc.vector.quantize_mx(out=codes[:].bitcast(FP8X4), scales=scales[:], in_=grouped)
+            return codes, scales
+
+        def product(acc, weights, t, moving):
+            cols = slice(P * t, P * (t + 1))
+            nc.tensor.matmul_mx(
+                out=acc,
+                lhsT=weights[0][:, cols].bitcast(FP8X4),
+                lhsT_scale=weights[1][:, cols],
+                rhs=moving[0].bitcast(FP8X4),
+                rhs_scale=moving[1],
+                start=True,
+                stop=True,
+            )
+
+        w1_grouped = sb("w1_grouped", [P, PACK * D], BF16, "stage0")
+        dst, src = deal_views(w1_grouped, w1_raw, 0, W1_VECTOR_SHARE)
+        nc.vector.tensor_copy(dst, src)
+        dst, src = deal_views(w1_grouped, w1_raw, W1_VECTOR_SHARE, P)
+        nc.scalar.copy(dst, src)
+        w1_q = quantized("w1", w1_grouped[:], D)
+        x_scale_picked = sb("x_scale_picked", [P, S], U8, "stage0")
+        nc.vector.tensor_copy(x_scale_picked[:], x_scale_table[:].indirect(offs_sb[:]))
+        seed_sb = sb("seed_sb", [P, PACK, S], F32, "big0")
+        for u in range(2):
+            nc.sync.dma_start(seed_sb[:, 2 * u : 2 * u + 2, :], rows_dealt(seed)[:, 2 * u : 2 * u + 2, :])
+        kn_sb = sb("kn_sb", [P, S], F32, "small")
+        nc.sync.dma_start(kn_sb[:], kn)
+
+        def seed_rows(t):
+            return seed_sb[:, t, :]
+
+        y = [sb(f"y{t}", [P, S], F32) for t in range(PACK)]
+        y_acc = {}
+        for h in range(2):
+            picked = sb(f"x_word_picked{h}", [P, HALF], U32, f"picked{h}")
+            nc.vector.tensor_copy(
+                picked[:], x_word_table[:].indirect(offs_sb[:, h * HALF // 16 : (h + 1) * HALF // 16])
+            )
+            for t in range(PACK):
+                y_acc[t, h] = bank(f"y_acc{t}{h}", [P, HALF])
+                product(y_acc[t, h][:], w1_q, t, (picked[:], x_scale_picked[:, h * HALF : (h + 1) * HALF]))
+        for t, h in ((0, 0), (1, 0), (0, 1), (1, 1), (2, 0), (2, 1), (3, 0), (3, 1)):
+            nc.scalar.activation(y[t][:, h * HALF : (h + 1) * HALF], y_acc[t, h][:], ACT.Copy, scale=0.75)
+
+        gn_sb = sb("gn_sb", [P, PACK], F32, "picked0")
+        nc.sync.dma_start(gn_sb[:], gn.rearrange("(p t) o -> p (t o)", t=PACK))
+        w2_raw = load_rows("w2_raw", w2, "big1")
+        unknown = sb("unknown", [P, S], F32)
+        nc.scalar.activation(unknown[:], kn_sb[:], ACT.Copy, scale=-1.0, bias=1.0)
+        seed_gained = sb("seed_gained", [P, PACK, S], F32)
+        for t in range(PACK):
+            nc.scalar.activation(seed_gained[:, t, :], seed_rows(t), ACT.Copy, scale=gn_sb[:, t : t + 1])
+        w2_grouped = sb("w2_grouped", [P, PACK * D], BF16, "stage1")
+        nc.scalar.copy(*deal_views(w2_grouped, w2_raw, 0, P))
+        w3_raw = load_rows("w3_raw", w3, "big1")
+        gain_rows = sb("gain_rows", [P, PACK, HALF], F32)
+
+        def woven(ap):
+            return ap.rearrange("p t (c i) -> p c t i", i=PACK)
+
+        def woven_out(tile):
+            return tile[:].rearrange("p (c i t) -> p c t i", i=PACK, t=PACK)
+
+        hid = [sb(f"hid{t}", [P, S], F32) for t in range(PACK)]
+        w2_q = None
+        w3_q = None
+        for ci, (c0, n) in enumerate(CHUNKS):
+            cols = slice(c0, c0 + n)
+            lcols = slice(c0 // 16, (c0 + n) // 16)
+            first = sb(f"first{ci}", [P, PACK, n], F32, "first")
+            both = sb(f"both{ci}", [P, PACK, n], F32, "both")
+            pull = both
+
+            def gather_first(t):
+                nc.vector.tensor_tensor(
+                    first[:, t, :], y[t][:].indirect(e1_sb[:, lcols]), seed_rows(t)[:, cols], ALU.subtract
+                )
+
+            def gather_second(t):
+                nc.vector.tensor_tensor(
+                    both[:, t, :], y[t][:].indirect(e2_sb[:, lcols]), first[:, t, :], ALU.add
+                )
+
+            gather_first(0)
+            for t in range(1, PACK):
+                gather_first(t)
+                gather_second(t - 1)
+            for t in range(PACK):
+                if t == 1:
+                    gather_second(PACK - 1)
+                nc.vector.scalar_tensor_tensor(
+                    pull[:, t, :], both[:, t, :], gn_sb[:, t : t + 1], unknown[:, cols], ALU.mult, ALU.mult
+                )
+            if ci == 0:
+                w2_q = quantized("w2", w2_grouped[:], D)
+            z_grouped = sb(f"z_grouped{ci}", [P, PACK * n], BF16, ("stage0", "stage1", "stage1")[ci])
+            nc.vector.tensor_tensor(woven_out(z_grouped), woven(pull[:]), woven(seed_gained[:, :, cols]), ALU.add)
+            z_q = quantized(f"z{ci}", z_grouped[:], n)
+            for t in range(PACK):
+                acc = bank(f"h_acc{ci}{t}", [P, n])
+                product(acc[:], w2_q, t, (z_q[0][:], z_q[1][:]))
+                nc.scalar.activation(hid[t][:, cols], acc[:], ACT.Tanh)
+            if ci == 0:
+                w3_grouped = sb("w3_grouped", [P, PACK * D], BF16, "stage0")
+                nc.scalar.copy(*deal_views(w3_grouped, w3_raw, 0, P))
+                nc.scalar.copy(gain_rows[:], gn_sb[:].unsqueeze(2).to_broadcast([P, PACK, HALF]))
+        res_sb = load_rows("res_sb", res, "big0")
+        w3_q = quantized("w3", w3_grouped[:], D)
+
+        out_rows = rows_dealt(out)
+        moved = []
+        z2_grouped = []
+
+        def gather_chunk(ci):
+            c0, n = CHUNKS[ci]
+            lcols = slice(c0 // 16, (c0 + n) // 16)
+            tile = sb(f"moved{ci}", [P, PACK, n], F32)
+            for t in range(PACK):
+                nc.vector.tensor_tensor(
+                    tile[:, t, :], hid[t][:].indirect(mv_sb[:, lcols]), gain_rows[:, t, 0:n], ALU.mult
+                )
+            grouped = sb(f"z2_grouped{ci}", [P, PACK * n], BF16)
+            nc.scalar.copy(woven_out(grouped), woven(tile[:]))
+            z2_grouped.append(grouped)
+
+        accs = {}
+
+        def multiply_chunk(ci):
+            c0, n = CHUNKS[ci]
+            z2_q = quantized(f"z2{ci}", z2_grouped[ci][:], n)
+            per_bank = S // n
+            for t0 in range(0, PACK, per_bank):
+                acc = bank(f"o_acc{ci}{t0}", [P, per_bank, n])
+                for t in range(t0, t0 + per_bank):
+                    product(acc[:, t - t0, :], w3_q, t, (z2_q[0][:], z2_q[1][:]))
+                accs[ci, t0] = acc
+
+        def finish_chunk(ci):
+            c0, n = CHUNKS[ci]
+            cols = slice(c0, c0 + n)
+            per_bank = S // n
+            for t0 in range(0, PACK, per_bank):
+                ts = slice(t0, t0 + per_bank)
+                result = sb(f"result{ci}{t0}", [P, per_bank, n], F32)
+                nc.vector.tensor_tensor(result[:], accs[ci, t0][:], res_sb[:, ts, cols], ALU.add)
+                nc.sync.dma_start(out_rows[:, ts, cols], result[:])
+
+        gather_chunk(0)
+        gather_chunk(1)
+        multiply_chunk(0)
+        gather_chunk(2)
+        multiply_chunk(1)
+        finish_chunk(0)
+        multiply_chunk(2)
+        finish_chunk(1)
+        finish_chunk(2)

@@ -18,8 +18,9 @@ T = 2048
 S = 512
 D = 512
 HALF = S // 2
-CHUNKS = ((0, 256), (256, 128), (384, 128))
-W1_VECTOR_SHARE = 80
+MOVE_SLICES = ((0, 384), (384, 128))
+OUT_CHUNKS = ((0, 256), (256, 128), (384, 128))
+W1_VECTOR_SHARE = 44
 
 FLOPS = 3 * 2 * D * D * S
 
@@ -46,28 +47,42 @@ def tile_picked_clampprop_none_p_kernel(
             nc.sync.dma_start(tile[:], dram)
             return tile
 
-        def load_rows(name, dram, tag):
-            tile = sb(name, [P, PACK, D], F32, tag)
+        def load_rows(name, dram):
+            tile = sb(name, [P, PACK, D], F32)
             nc.sync.dma_start(tile[:], rows_dealt(dram))
             return tile
 
-        x_scale_table = sb("x_scale_table", [P, T], U8, "small")
+        x_scale_table = sb("x_scale_table", [P, T], U8)
         nc.gpsimd.memset(x_scale_table[:, 0 : T // 2].bitcast(I32), 0)
         nc.vector.memset(x_scale_table[:, T // 2 : T].bitcast(I32), 0)
+        offs_sb = load_list("offs_sb", offs)
+        e1_sb = load_list("e1_sb", e1)
+        w1_raw = load_rows("w1_raw", w1)
+        e2_sb = load_list("e2_sb", e2)
+        mv_sb = load_list("mv_sb", mv)
         for q in range(4):
-            nc.scalar.dma_start(
+            nc.sync.dma_start(
                 x_scale_table[32 * q : 32 * q + 4, :].bitcast(I32),
                 x_scales[0, 4 * q : 4 * q + 4, :].bitcast(I32),
             )
-        offs_sb = load_list("offs_sb", offs)
-        e1_sb = load_list("e1_sb", e1)
-        w1_raw = load_rows("w1_raw", w1, "big0")
-        x_word_table = sb("x_word_table", [P, T], U32, "big1")
+        x_word_table = sb("x_word_table", [P, T], U32)
         nc.sync.dma_start(
             x_word_table[:].bitcast(I32), x_words[0].rearrange("p n t -> p (n t)").bitcast(I32)
         )
-        e2_sb = load_list("e2_sb", e2)
-        mv_sb = load_list("mv_sb", mv)
+        seed_sb = sb("seed_sb", [P, PACK, S], F32)
+        nc.sync.dma_start(seed_sb[:, 0:2, :], rows_dealt(seed)[:, 0:2, :])
+        kn_sb = sb("kn_sb", [P, S], F32)
+        nc.sync.dma_start(kn_sb[:], kn)
+        gn_sb = sb("gn_sb", [P, PACK], F32)
+        nc.sync.dma_start(gn_sb[:], gn.rearrange("(p t) o -> p (t o)", t=PACK))
+        nc.sync.dma_start(seed_sb[:, 2:4, :], rows_dealt(seed)[:, 2:4, :])
+        w2_raw = load_rows("w2_raw", w2)
+        w3_raw = load_rows("w3_raw", w3)
+        res_sb = load_rows("res_sb", res)
+
+        y = [sb(f"y{t}", [P, 2 * S], F32) for t in range(PACK)]
+        for t in range(PACK):
+            nc.gpsimd.memset(y[t][:, S : 2 * S], 0.0)
 
         def deal_views(grouped, raw, m0, m1):
             dst = grouped[:].rearrange("p (t m j) -> p m j t", t=PACK, j=PACK)[:, m0:m1]
@@ -92,27 +107,22 @@ def tile_picked_clampprop_none_p_kernel(
                 stop=True,
             )
 
-        w1_grouped = sb("w1_grouped", [P, PACK * D], BF16, "stage0")
-        dst, src = deal_views(w1_grouped, w1_raw, 0, W1_VECTOR_SHARE)
-        nc.vector.tensor_copy(dst, src)
-        dst, src = deal_views(w1_grouped, w1_raw, W1_VECTOR_SHARE, P)
-        nc.scalar.copy(dst, src)
-        w1_q = quantized("w1", w1_grouped[:], D)
-        x_scale_picked = sb("x_scale_picked", [P, S], U8, "stage0")
+        def woven(ap):
+            return ap.rearrange("p t (c i) -> p c t i", i=PACK)
+
+        def woven_out(tile):
+            return tile[:].rearrange("p (c i t) -> p c t i", i=PACK, t=PACK)
+
+        w1_grouped = sb("w1_grouped", [P, PACK * D], BF16, "w1_stage")
+        nc.vector.tensor_copy(*deal_views(w1_grouped, w1_raw, 0, W1_VECTOR_SHARE))
+        nc.scalar.copy(*deal_views(w1_grouped, w1_raw, W1_VECTOR_SHARE, P))
+        x_scale_picked = sb("x_scale_picked", [P, S], U8)
         nc.vector.tensor_copy(x_scale_picked[:], x_scale_table[:].indirect(offs_sb[:]))
-        seed_sb = sb("seed_sb", [P, PACK, S], F32, "big0")
-        for u in range(2):
-            nc.sync.dma_start(seed_sb[:, 2 * u : 2 * u + 2, :], rows_dealt(seed)[:, 2 * u : 2 * u + 2, :])
-        kn_sb = sb("kn_sb", [P, S], F32, "small")
-        nc.sync.dma_start(kn_sb[:], kn)
+        w1_q = quantized("w1", w1_grouped[:], D)
 
-        def seed_rows(t):
-            return seed_sb[:, t, :]
-
-        y = [sb(f"y{t}", [P, S], F32) for t in range(PACK)]
         y_acc = {}
         for h in range(2):
-            picked = sb(f"x_word_picked{h}", [P, HALF], U32, f"picked{h}")
+            picked = sb(f"x_word_picked{h}", [P, HALF], U32, ("w1_stage", None)[h])
             nc.vector.tensor_copy(
                 picked[:], x_word_table[:].indirect(offs_sb[:, h * HALF // 16 : (h + 1) * HALF // 16])
             )
@@ -122,115 +132,79 @@ def tile_picked_clampprop_none_p_kernel(
         for t, h in ((0, 0), (1, 0), (0, 1), (1, 1), (2, 0), (2, 1), (3, 0), (3, 1)):
             nc.scalar.activation(y[t][:, h * HALF : (h + 1) * HALF], y_acc[t, h][:], ACT.Copy, scale=0.75)
 
-        gn_sb = sb("gn_sb", [P, PACK], F32, "picked0")
-        nc.sync.dma_start(gn_sb[:], gn.rearrange("(p t) o -> p (t o)", t=PACK))
-        w2_raw = load_rows("w2_raw", w2, "big1")
         unknown = sb("unknown", [P, S], F32)
         nc.scalar.activation(unknown[:], kn_sb[:], ACT.Copy, scale=-1.0, bias=1.0)
         seed_gained = sb("seed_gained", [P, PACK, S], F32)
         for t in range(PACK):
-            nc.scalar.activation(seed_gained[:, t, :], seed_rows(t), ACT.Copy, scale=gn_sb[:, t : t + 1])
-        w2_grouped = sb("w2_grouped", [P, PACK * D], BF16, "stage1")
+            nc.scalar.activation(seed_gained[:, t, :], seed_sb[:, t, :], ACT.Copy, scale=gn_sb[:, t : t + 1])
+        w2_grouped = sb("w2_grouped", [P, PACK * D], BF16, "stage")
         nc.scalar.copy(*deal_views(w2_grouped, w2_raw, 0, P))
-        w3_raw = load_rows("w3_raw", w3, "big1")
-        gain_rows = sb("gain_rows", [P, PACK, HALF], F32)
+        w3_grouped = sb("w3_grouped", [P, PACK * D], BF16)
+        nc.scalar.copy(*deal_views(w3_grouped, w3_raw, 0, P))
+        widest = MOVE_SLICES[0][1]
+        gain_rows = sb("gain_rows", [P, PACK, widest], F32)
+        nc.scalar.copy(gain_rows[:], gn_sb[:].unsqueeze(2).to_broadcast([P, PACK, widest]))
 
-        def woven(ap):
-            return ap.rearrange("p t (c i) -> p c t i", i=PACK)
+        first = sb("first", [P, PACK, S], F32)
+        pull = sb("pull", [P, PACK, S], F32)
 
-        def woven_out(tile):
-            return tile[:].rearrange("p (c i t) -> p c t i", i=PACK, t=PACK)
+        def gather_first(t):
+            nc.vector.tensor_tensor(first[:, t, :], y[t][:].indirect(e1_sb[:]), seed_sb[:, t, :], ALU.subtract)
+
+        def gather_second(t):
+            nc.vector.tensor_tensor(pull[:, t, :], y[t][:].indirect(e2_sb[:]), first[:, t, :], ALU.add)
+
+        def weigh(t):
+            nc.vector.scalar_tensor_tensor(
+                pull[:, t, :], pull[:, t, :], gn_sb[:, t : t + 1], unknown[:], ALU.mult, ALU.mult
+            )
+
+        for step in range(PACK + 2):
+            if step < PACK:
+                gather_first(step)
+            if 1 <= step <= PACK:
+                gather_second(step - 1)
+            if step == PACK + 1:
+                w2_q = quantized("w2", w2_grouped[:], D)
+            if step >= 2:
+                weigh(step - 2)
 
         hid = [sb(f"hid{t}", [P, S], F32) for t in range(PACK)]
-        w2_q = None
-        w3_q = None
-        for ci, (c0, n) in enumerate(CHUNKS):
-            cols = slice(c0, c0 + n)
-            lcols = slice(c0 // 16, (c0 + n) // 16)
-            first = sb(f"first{ci}", [P, PACK, n], F32, "first")
-            both = sb(f"both{ci}", [P, PACK, n], F32, "both")
-            pull = both
-
-            def gather_first(t):
-                nc.vector.tensor_tensor(
-                    first[:, t, :], y[t][:].indirect(e1_sb[:, lcols]), seed_rows(t)[:, cols], ALU.subtract
-                )
-
-            def gather_second(t):
-                nc.vector.tensor_tensor(
-                    both[:, t, :], y[t][:].indirect(e2_sb[:, lcols]), first[:, t, :], ALU.add
-                )
-
-            gather_first(0)
-            for t in range(1, PACK):
-                gather_first(t)
-                gather_second(t - 1)
+        for h in range(2):
+            cols = slice(h * HALF, (h + 1) * HALF)
+            z_grouped = sb(f"z_grouped{h}", [P, PACK * HALF], BF16, "stage")
+            nc.vector.tensor_tensor(woven_out(z_grouped), woven(pull[:, :, cols]), woven(seed_gained[:, :, cols]), ALU.add)
+            z_q = quantized(f"z{h}", z_grouped[:], HALF)
             for t in range(PACK):
-                if t == 1:
-                    gather_second(PACK - 1)
-                nc.vector.scalar_tensor_tensor(
-                    pull[:, t, :], both[:, t, :], gn_sb[:, t : t + 1], unknown[:, cols], ALU.mult, ALU.mult
-                )
-            if ci == 0:
-                w2_q = quantized("w2", w2_grouped[:], D)
-            z_grouped = sb(f"z_grouped{ci}", [P, PACK * n], BF16, ("stage0", "stage1", "stage1")[ci])
-            nc.vector.tensor_tensor(woven_out(z_grouped), woven(pull[:]), woven(seed_gained[:, :, cols]), ALU.add)
-            z_q = quantized(f"z{ci}", z_grouped[:], n)
-            for t in range(PACK):
-                acc = bank(f"h_acc{ci}{t}", [P, n])
+                acc = bank(f"h_acc{h}{t}", [P, HALF])
                 product(acc[:], w2_q, t, (z_q[0][:], z_q[1][:]))
                 nc.scalar.activation(hid[t][:, cols], acc[:], ACT.Tanh)
-            if ci == 0:
-                w3_grouped = sb("w3_grouped", [P, PACK * D], BF16, "stage0")
-                nc.scalar.copy(*deal_views(w3_grouped, w3_raw, 0, P))
-                nc.scalar.copy(gain_rows[:], gn_sb[:].unsqueeze(2).to_broadcast([P, PACK, HALF]))
-        res_sb = load_rows("res_sb", res, "big0")
         w3_q = quantized("w3", w3_grouped[:], D)
 
         out_rows = rows_dealt(out)
-        moved = []
-        z2_grouped = []
-
-        def gather_chunk(ci):
-            c0, n = CHUNKS[ci]
-            lcols = slice(c0 // 16, (c0 + n) // 16)
-            tile = sb(f"moved{ci}", [P, PACK, n], F32)
+        moved = {}
+        for c0, n in MOVE_SLICES:
+            moved[c0] = sb(f"moved{c0}", [P, PACK, n], F32)
             for t in range(PACK):
                 nc.vector.tensor_tensor(
-                    tile[:, t, :], hid[t][:].indirect(mv_sb[:, lcols]), gain_rows[:, t, 0:n], ALU.mult
+                    moved[c0][:, t, :],
+                    hid[t][:].indirect(mv_sb[:, c0 // 16 : (c0 + n) // 16]),
+                    gain_rows[:, t, 0:n],
+                    ALU.mult,
                 )
-            grouped = sb(f"z2_grouped{ci}", [P, PACK * n], BF16)
-            nc.scalar.copy(woven_out(grouped), woven(tile[:]))
-            z2_grouped.append(grouped)
-
-        accs = {}
-
-        def multiply_chunk(ci):
-            c0, n = CHUNKS[ci]
-            z2_q = quantized(f"z2{ci}", z2_grouped[ci][:], n)
-            per_bank = S // n
+        accs = []
+        for c0, n in OUT_CHUNKS:
+            z2_grouped = sb(f"z2_grouped{c0}", [P, PACK * n], BF16)
+            m0 = max(s0 for s0, width in MOVE_SLICES if s0 <= c0)
+            nc.scalar.copy(woven_out(z2_grouped), woven(moved[m0][:, :, c0 - m0 : c0 - m0 + n]))
+            z2_q = quantized(f"z2{c0}", z2_grouped[:], n)
+            per_bank = 2 if c0 + n == S else S // n
             for t0 in range(0, PACK, per_bank):
-                acc = bank(f"o_acc{ci}{t0}", [P, per_bank, n])
+                acc = bank(f"o_acc{c0}{t0}", [P, per_bank, n])
                 for t in range(t0, t0 + per_bank):
                     product(acc[:, t - t0, :], w3_q, t, (z2_q[0][:], z2_q[1][:]))
-                accs[ci, t0] = acc
-
-        def finish_chunk(ci):
-            c0, n = CHUNKS[ci]
-            cols = slice(c0, c0 + n)
-            per_bank = S // n
-            for t0 in range(0, PACK, per_bank):
-                ts = slice(t0, t0 + per_bank)
-                result = sb(f"result{ci}{t0}", [P, per_bank, n], F32)
-                nc.vector.tensor_tensor(result[:], accs[ci, t0][:], res_sb[:, ts, cols], ALU.add)
-                nc.sync.dma_start(out_rows[:, ts, cols], result[:])
-
-        gather_chunk(0)
-        gather_chunk(1)
-        multiply_chunk(0)
-        gather_chunk(2)
-        multiply_chunk(1)
-        finish_chunk(0)
-        multiply_chunk(2)
-        finish_chunk(1)
-        finish_chunk(2)
+                accs.append((acc, slice(t0, t0 + per_bank), slice(c0, c0 + n)))
+        for b, (acc, ts, cols) in enumerate(accs):
+            result = sb(f"result{b}", list(acc.shape), F32)
+            nc.vector.tensor_tensor(result[:], acc[:], res_sb[:, ts, cols], ALU.add)
+            nc.sync.dma_start(out_rows[:, ts, cols], result[:])

@@ -1,6 +1,7 @@
 from contextlib import ExitStack
 
 import concourse.mybir as mybir
+from concourse.masks import make_identity
 
 F32 = mybir.dt.float32
 BF16 = mybir.dt.bfloat16
@@ -18,9 +19,9 @@ T = 2048
 S = 512
 D = 512
 HALF = S // 2
+BLOCKS = S // P
 MOVE_SLICES = ((0, 384), (384, 128))
-OUT_CHUNKS = ((0, 256), (256, 128), (384, 128))
-W1_VECTOR_SHARE = 44
+CHUNKS = ((0, 256), (256, 128), (384, 128))
 
 FLOPS = 3 * 2 * D * D * S
 
@@ -31,13 +32,13 @@ def tile_picked_clampprop_none_p_kernel(
     nc = tc.nc
     with ExitStack() as ctx:
         keep = ctx.enter_context(tc.tile_pool(name="keep", bufs=1))
-        psum = ctx.enter_context(tc.psum_pool(name="psum", bufs=8))
+        psum = ctx.enter_context(tc.psum_pool(name="psum", bufs=1))
 
         def sb(name, shape, dtype, tag=None):
             return keep.tile(shape, dtype, name=name, tag=tag or name, align_bytes=64)
 
-        def bank(name, shape):
-            return psum.tile(shape, F32, name=name, tag="bank")
+        def bank(name, shape, number):
+            return psum.tile(shape, F32, name=name, tag=f"bank{number}")
 
         def rows_dealt(dram):
             return dram.rearrange("(p t) c -> p t c", t=PACK)
@@ -56,10 +57,11 @@ def tile_picked_clampprop_none_p_kernel(
         nc.gpsimd.memset(x_scale_table[:, 0 : T // 2].bitcast(I32), 0)
         nc.vector.memset(x_scale_table[:, T // 2 : T].bitcast(I32), 0)
         offs_sb = load_list("offs_sb", offs)
-        e1_sb = load_list("e1_sb", e1)
+        gn_sb = sb("gn_sb", [P, PACK], F32)
+        nc.sync.dma_start(gn_sb[:], gn.rearrange("(p t) o -> p (t o)", t=PACK))
         w1_raw = load_rows("w1_raw", w1)
+        e1_sb = load_list("e1_sb", e1)
         e2_sb = load_list("e2_sb", e2)
-        mv_sb = load_list("mv_sb", mv)
         for q in range(4):
             nc.sync.dma_start(
                 x_scale_table[32 * q : 32 * q + 4, :].bitcast(I32),
@@ -69,30 +71,43 @@ def tile_picked_clampprop_none_p_kernel(
         nc.sync.dma_start(
             x_word_table[:].bitcast(I32), x_words[0].rearrange("p n t -> p (n t)").bitcast(I32)
         )
-        seed_sb = sb("seed_sb", [P, PACK, S], F32)
-        nc.sync.dma_start(seed_sb[:, 0:2, :], rows_dealt(seed)[:, 0:2, :])
-        kn_sb = sb("kn_sb", [P, S], F32)
-        nc.sync.dma_start(kn_sb[:], kn)
-        gn_sb = sb("gn_sb", [P, PACK], F32)
-        nc.sync.dma_start(gn_sb[:], gn.rearrange("(p t) o -> p (t o)", t=PACK))
-        nc.sync.dma_start(seed_sb[:, 2:4, :], rows_dealt(seed)[:, 2:4, :])
+        seed_sb = load_rows("seed_sb", seed)
+        known = sb("known", [P, BLOCKS], F32)
+        with nc.allow_non_contiguous_dma(reason="one value of kn a partition and block"):
+            nc.sync.dma_start(known[:], kn[0:1, :].rearrange("o (b p) -> p (o b)", p=P))
         w2_raw = load_rows("w2_raw", w2)
+        mv_sb = load_list("mv_sb", mv)
         w3_raw = load_rows("w3_raw", w3)
         res_sb = load_rows("res_sb", res)
 
         y = [sb(f"y{t}", [P, 2 * S], F32) for t in range(PACK)]
         for t in range(PACK):
             nc.gpsimd.memset(y[t][:, S : 2 * S], 0.0)
+        identity = sb("identity", [P, P], F32)
+        make_identity(nc, identity[:])
+        widest = MOVE_SLICES[0][1]
+        last = PACK - 1
+        gain_rows = sb("gain_rows", [P, last, widest], F32)
+        nc.vector.tensor_copy(gain_rows[:], gn_sb[:, 0:last].unsqueeze(2).to_broadcast([P, last, widest]))
+        gain_last = {}
+        for s0, width in MOVE_SLICES:
+            gain_last[s0] = sb(f"gain_last{s0}", [P, width], F32)
+            nc.vector.tensor_copy(gain_last[s0][:], gn_sb[:, last:PACK].to_broadcast([P, width]))
 
-        def deal_views(grouped, raw, m0, m1):
-            dst = grouped[:].rearrange("p (t m j) -> p m j t", t=PACK, j=PACK)[:, m0:m1]
-            src = raw[:].rearrange("p j (m t) -> p m j t", t=PACK)[:, m0:m1]
+        def deal_views(grouped, raw, t0, t1):
+            dst = grouped[:].rearrange("p (t m j) -> p m j t", m=P, j=PACK)
+            src = raw[:].rearrange("p j (m t) -> p m j t", t=PACK)[:, :, :, t0:t1]
             return dst, src
 
+        def quantize(codes, scales, grouped):
+            nc.vector.quantize_mx(out=codes.bitcast(FP8X4), scales=scales, in_=grouped)
+
+        def mx_tiles(name, width):
+            return sb(name + "_codes", [P, width], U32), sb(name + "_scales", [P, width], U8)
+
         def quantized(name, grouped, width):
-            codes = sb(name + "_codes", [P, width], U32)
-            scales = sb(name + "_scales", [P, width], U8)
-            nc.vector.quantize_mx(out=codes[:].bitcast(FP8X4), scales=scales[:], in_=grouped)
+            codes, scales = mx_tiles(name, width)
+            quantize(codes[:], scales[:], grouped)
             return codes, scales
 
         def product(acc, weights, t, moving):
@@ -113,94 +128,117 @@ def tile_picked_clampprop_none_p_kernel(
         def woven_out(tile):
             return tile[:].rearrange("p (c i t) -> p c t i", i=PACK, t=PACK)
 
-        w1_grouped = sb("w1_grouped", [P, PACK * D], BF16, "w1_stage")
-        nc.vector.tensor_copy(*deal_views(w1_grouped, w1_raw, 0, W1_VECTOR_SHARE))
-        nc.scalar.copy(*deal_views(w1_grouped, w1_raw, W1_VECTOR_SHARE, P))
+        w1_low = sb("w1_low", [P, 2 * D], BF16, "w1_low")
+        w1_high = sb("w1_high", [P, 2 * D], BF16, "w1_high")
+        nc.vector.tensor_copy(*deal_views(w1_low, w1_raw, 0, 2))
+        nc.scalar.copy(*deal_views(w1_high, w1_raw, 2, 4))
         x_scale_picked = sb("x_scale_picked", [P, S], U8)
         nc.vector.tensor_copy(x_scale_picked[:], x_scale_table[:].indirect(offs_sb[:]))
-        w1_q = quantized("w1", w1_grouped[:], D)
+        w1_q = mx_tiles("w1", D)
+        for u, grouped in enumerate((w1_low, w1_high)):
+            cols = slice(u * D // 2, (u + 1) * D // 2)
+            quantize(w1_q[0][:, cols], w1_q[1][:, cols], grouped[:])
 
-        y_acc = {}
+        picked = []
         for h in range(2):
-            picked = sb(f"x_word_picked{h}", [P, HALF], U32, ("w1_stage", None)[h])
+            tile = sb(f"x_word_picked{h}", [P, HALF], U32, ("w1_high", "w1_low")[h])
             nc.vector.tensor_copy(
-                picked[:], x_word_table[:].indirect(offs_sb[:, h * HALF // 16 : (h + 1) * HALF // 16])
+                tile[:], x_word_table[:].indirect(offs_sb[:, h * HALF // 16 : (h + 1) * HALF // 16])
             )
-            for t in range(PACK):
-                y_acc[t, h] = bank(f"y_acc{t}{h}", [P, HALF])
-                product(y_acc[t, h][:], w1_q, t, (picked[:], x_scale_picked[:, h * HALF : (h + 1) * HALF]))
-        for t, h in ((0, 0), (1, 0), (0, 1), (1, 1), (2, 0), (2, 1), (3, 0), (3, 1)):
-            nc.scalar.activation(y[t][:, h * HALF : (h + 1) * HALF], y_acc[t, h][:], ACT.Copy, scale=0.75)
+            picked.append(tile)
+        for number, (t, h) in enumerate(((0, 0), (1, 0), (0, 1), (1, 1), (2, 0), (2, 1), (3, 0), (3, 1))):
+            cols = slice(h * HALF, (h + 1) * HALF)
+            acc = bank(f"y_acc{t}{h}", [P, HALF], number)
+            product(acc[:], w1_q, t, (picked[h][:], x_scale_picked[:, cols]))
+            nc.scalar.activation(y[t][:, cols], acc[:], ACT.Copy, scale=gn_sb[:, t : t + 1])
 
-        unknown = sb("unknown", [P, S], F32)
-        nc.scalar.activation(unknown[:], kn_sb[:], ACT.Copy, scale=-1.0, bias=1.0)
         seed_gained = sb("seed_gained", [P, PACK, S], F32)
         for t in range(PACK):
             nc.scalar.activation(seed_gained[:, t, :], seed_sb[:, t, :], ACT.Copy, scale=gn_sb[:, t : t + 1])
-        w2_grouped = sb("w2_grouped", [P, PACK * D], BF16, "stage")
-        nc.scalar.copy(*deal_views(w2_grouped, w2_raw, 0, P))
+        spread = sb("spread", [P, BLOCKS], F32)
+        nc.scalar.activation(spread[:], known[:], ACT.Copy, scale=-0.75, bias=0.75)
+
+        def by_feature(turned):
+            return turned[:].rearrange("r t p -> r p t")
+
+        held = []
+        for b in range(BLOCKS):
+            turned = bank(f"seed_turned{b}", [P, PACK, P], b)
+            for t in range(PACK):
+                nc.tensor.transpose(turned[:, t, :], seed_gained[:, t, P * b : P * (b + 1)], identity[:])
+            tile = sb(f"held{b}", [P, P, PACK], F32)
+            nc.scalar.activation(tile[:], by_feature(turned), ACT.Copy, scale=known[:, b : b + 1])
+            held.append(tile)
+        w2_grouped = sb("w2_grouped", [P, PACK * D], BF16)
+        nc.scalar.copy(*deal_views(w2_grouped, w2_raw, 0, PACK))
         w3_grouped = sb("w3_grouped", [P, PACK * D], BF16)
-        nc.scalar.copy(*deal_views(w3_grouped, w3_raw, 0, P))
-        widest = MOVE_SLICES[0][1]
-        gain_rows = sb("gain_rows", [P, PACK, widest], F32)
-        nc.scalar.copy(gain_rows[:], gn_sb[:].unsqueeze(2).to_broadcast([P, PACK, widest]))
+        nc.scalar.copy(*deal_views(w3_grouped, w3_raw, 0, PACK))
 
         first = sb("first", [P, PACK, S], F32)
-        pull = sb("pull", [P, PACK, S], F32)
-
-        def gather_first(t):
-            nc.vector.tensor_tensor(first[:, t, :], y[t][:].indirect(e1_sb[:]), seed_sb[:, t, :], ALU.subtract)
-
-        def gather_second(t):
-            nc.vector.tensor_tensor(pull[:, t, :], y[t][:].indirect(e2_sb[:]), first[:, t, :], ALU.add)
-
-        def weigh(t):
-            nc.vector.scalar_tensor_tensor(
-                pull[:, t, :], pull[:, t, :], gn_sb[:, t : t + 1], unknown[:], ALU.mult, ALU.mult
-            )
-
-        for step in range(PACK + 2):
+        both = sb("both", [P, PACK, S], F32)
+        both_turned = [bank(f"both_turned{b}", [P, PACK, P], b) for b in range(BLOCKS)]
+        for step in range(PACK + 1):
             if step < PACK:
-                gather_first(step)
-            if 1 <= step <= PACK:
-                gather_second(step - 1)
-            if step == PACK + 1:
-                w2_q = quantized("w2", w2_grouped[:], D)
-            if step >= 2:
-                weigh(step - 2)
+                nc.vector.tensor_copy(first[:, step, :], y[step][:].indirect(e1_sb[:]))
+            if step >= 1:
+                t = step - 1
+                nc.vector.tensor_tensor(both[:, t, :], y[t][:].indirect(e2_sb[:]), first[:, t, :], ALU.add)
+                for b in range(BLOCKS):
+                    nc.tensor.transpose(both_turned[b][:, t, :], both[:, t, P * b : P * (b + 1)], identity[:])
+        w2_q = quantized("w2", w2_grouped[:], D)
+
+        z_grouped = {c0: sb(f"z_grouped{c0}", [P, PACK * n], BF16) for c0, n in CHUNKS}
+        for b in range(BLOCKS):
+            z_turned = sb(f"z_turned{b}", [P, P, PACK], BF16)
+            nc.vector.scalar_tensor_tensor(
+                z_turned[:], by_feature(both_turned[b]), spread[:, b : b + 1], held[b][:], ALU.mult, ALU.add
+            )
+            pairs = z_turned[:].rearrange("r p t -> r (p t)").bitcast(F32)
+            pairs_back = bank(f"pairs_back{b}", [P, 2, P], BLOCKS + b)
+            for u in range(2):
+                nc.tensor.transpose(pairs_back[:, u, :], pairs[:, u : 2 * P : 2], identity[:])
+            c0 = max(start for start, width in CHUNKS if start <= P * b)
+            place = slice(2 * (P * b - c0), 2 * (P * (b + 1) - c0))
+            nc.scalar.copy(
+                z_grouped[c0][:].bitcast(F32)[:, place].rearrange("p (r u) -> p r u", u=2),
+                pairs_back[:].rearrange("p u r -> p r u"),
+            )
+        z_q = {c0: quantized(f"z{c0}", z_grouped[c0][:], n) for c0, n in CHUNKS}
+        w3_q = (sb("w3_codes", [P, D], U32, f"z_grouped{CHUNKS[-1][0]}"), sb("w3_scales", [P, D], U8))
+        quantize(w3_q[0][:], w3_q[1][:], w3_grouped[:])
 
         hid = [sb(f"hid{t}", [P, S], F32) for t in range(PACK)]
-        for h in range(2):
-            cols = slice(h * HALF, (h + 1) * HALF)
-            z_grouped = sb(f"z_grouped{h}", [P, PACK * HALF], BF16, "stage")
-            nc.vector.tensor_tensor(woven_out(z_grouped), woven(pull[:, :, cols]), woven(seed_gained[:, :, cols]), ALU.add)
-            z_q = quantized(f"z{h}", z_grouped[:], HALF)
-            for t in range(PACK):
-                acc = bank(f"h_acc{h}{t}", [P, HALF])
-                product(acc[:], w2_q, t, (z_q[0][:], z_q[1][:]))
-                nc.scalar.activation(hid[t][:, cols], acc[:], ACT.Tanh)
-        w3_q = quantized("w3", w3_grouped[:], D)
+        wide, narrow = MOVE_SLICES
+        for (s0, width), t, number in (
+            (wide, 0, 0), (narrow, 0, 4), (wide, 1, 1), (narrow, 1, 5),
+            (wide, 2, 4), (narrow, 2, 6), (wide, 3, 5), (narrow, 3, 7),
+        ):
+            acc = bank(f"h_acc{s0}{t}", [P, width], number)
+            for c0, n in CHUNKS:
+                if s0 <= c0 < s0 + width:
+                    product(acc[:, c0 - s0 : c0 - s0 + n], w2_q, t, (z_q[c0][0][:], z_q[c0][1][:]))
+            nc.scalar.activation(hid[t][:, s0 : s0 + width], acc[:], ACT.Tanh)
 
         out_rows = rows_dealt(out)
         moved = {}
         for c0, n in MOVE_SLICES:
-            moved[c0] = sb(f"moved{c0}", [P, PACK, n], F32)
+            moved[c0] = sb(f"moved{c0}", [P, PACK, n], F32, "gain_last0" if c0 else None)
             for t in range(PACK):
                 nc.vector.tensor_tensor(
                     moved[c0][:, t, :],
                     hid[t][:].indirect(mv_sb[:, c0 // 16 : (c0 + n) // 16]),
-                    gain_rows[:, t, 0:n],
+                    gain_last[c0][:] if t == last else gain_rows[:, t, 0:n],
                     ALU.mult,
                 )
         accs = []
-        for c0, n in OUT_CHUNKS:
+        for c0, n in CHUNKS:
             z2_grouped = sb(f"z2_grouped{c0}", [P, PACK * n], BF16)
-            m0 = max(s0 for s0, width in MOVE_SLICES if s0 <= c0)
+            m0 = max(start for start, width in MOVE_SLICES if start <= c0)
             nc.scalar.copy(woven_out(z2_grouped), woven(moved[m0][:, :, c0 - m0 : c0 - m0 + n]))
             z2_q = quantized(f"z2{c0}", z2_grouped[:], n)
             per_bank = 2 if c0 + n == S else S // n
             for t0 in range(0, PACK, per_bank):
-                acc = bank(f"o_acc{c0}{t0}", [P, per_bank, n])
+                acc = bank(f"o_acc{c0}{t0}", [P, per_bank, n], len(accs))
                 for t in range(t0, t0 + per_bank):
                     product(acc[:, t - t0, :], w3_q, t, (z2_q[0][:], z2_q[1][:]))
                 accs.append((acc, slice(t0, t0 + per_bank), slice(c0, c0 + n)))

@@ -72,17 +72,17 @@ def tile_picked_clampprop_none_p_kernel(
             x_word_table[:].bitcast(I32), x_words[0].rearrange("p n t -> p (n t)").bitcast(I32)
         )
         seed_sb = load_rows("seed_sb", seed)
+        w2_raw = load_rows("w2_raw", w2)
         known = sb("known", [P, BLOCKS], F32)
         with nc.allow_non_contiguous_dma(reason="one value of kn a partition and block"):
             nc.sync.dma_start(known[:], kn[0:1, :].rearrange("o (b p) -> p (o b)", p=P))
-        w2_raw = load_rows("w2_raw", w2)
         mv_sb = load_list("mv_sb", mv)
         w3_raw = load_rows("w3_raw", w3)
         res_sb = load_rows("res_sb", res)
 
         y = [sb(f"y{t}", [P, 2 * S], F32) for t in range(PACK)]
         for t in range(PACK):
-            nc.gpsimd.memset(y[t][:, S : 2 * S], 0.0)
+            nc.vector.memset(y[t][:, S : 2 * S], 0.0)
         identity = sb("identity", [P, P], F32)
         make_identity(nc, identity[:])
         widest = MOVE_SLICES[0][1]
@@ -150,7 +150,10 @@ def tile_picked_clampprop_none_p_kernel(
             cols = slice(h * HALF, (h + 1) * HALF)
             acc = bank(f"y_acc{t}{h}", [P, HALF], number)
             product(acc[:], w1_q, t, (picked[h][:], x_scale_picked[:, cols]))
-            nc.scalar.activation(y[t][:, cols], acc[:], ACT.Copy, scale=gn_sb[:, t : t + 1])
+            if number in (1, 2):
+                nc.vector.tensor_scalar(y[t][:, cols], acc[:], gn_sb[:, t : t + 1], None, ALU.mult)
+            else:
+                nc.scalar.activation(y[t][:, cols], acc[:], ACT.Copy, scale=gn_sb[:, t : t + 1])
 
         seed_gained = sb("seed_gained", [P, PACK, S], F32)
         for t in range(PACK):
@@ -171,8 +174,8 @@ def tile_picked_clampprop_none_p_kernel(
             held.append(tile)
         w2_grouped = sb("w2_grouped", [P, PACK * D], BF16)
         nc.scalar.copy(*deal_views(w2_grouped, w2_raw, 0, PACK))
-        w3_grouped = sb("w3_grouped", [P, PACK * D], BF16)
-        nc.scalar.copy(*deal_views(w3_grouped, w3_raw, 0, PACK))
+        w3_high = sb("w3_high", [P, 2 * D], BF16)
+        nc.scalar.copy(*deal_views(w3_high, w3_raw, 2, 4))
 
         first = sb("first", [P, PACK, S], F32)
         both = sb("both", [P, PACK, S], F32)
@@ -203,9 +206,16 @@ def tile_picked_clampprop_none_p_kernel(
                 z_grouped[c0][:].bitcast(F32)[:, place].rearrange("p (r u) -> p r u", u=2),
                 pairs_back[:].rearrange("p u r -> p r u"),
             )
-        z_q = {c0: quantized(f"z{c0}", z_grouped[c0][:], n) for c0, n in CHUNKS}
+        z_q = {}
+        for c0, n in CHUNKS:
+            if c0 + n == S:
+                w3_low = sb("w3_low", [P, 2 * D], BF16, f"z_grouped{CHUNKS[-2][0]}")
+                nc.vector.tensor_copy(*deal_views(w3_low, w3_raw, 0, 2))
+            z_q[c0] = quantized(f"z{c0}", z_grouped[c0][:], n)
         w3_q = (sb("w3_codes", [P, D], U32, f"z_grouped{CHUNKS[-1][0]}"), sb("w3_scales", [P, D], U8))
-        quantize(w3_q[0][:], w3_q[1][:], w3_grouped[:])
+        for u, grouped in enumerate((w3_low, w3_high)):
+            cols = slice(u * D // 2, (u + 1) * D // 2)
+            quantize(w3_q[0][:, cols], w3_q[1][:, cols], grouped[:])
 
         hid = [sb(f"hid{t}", [P, S], F32) for t in range(PACK)]
         wide, narrow = MOVE_SLICES

from contextlib import ExitStack

import concourse.mybir as mybir
from concourse.masks import make_identity

F32 = mybir.dt.float32
BF16 = mybir.dt.bfloat16
I32 = mybir.dt.int32
U32 = mybir.dt.uint32
U16 = mybir.dt.uint16
U8 = mybir.dt.uint8
FP8X4 = mybir.dt.float8_e4m3fn_x4
ALU = mybir.AluOpType
ACT = mybir.ActivationFunctionType

P = 128
PACK = 4
T = 2048
S = 512
D = 512
HALF = S // 2
BLOCKS = S // P
MOVE_SLICES = ((0, 384), (384, 128))
CHUNKS = ((0, 256), (256, 128), (384, 128))

FLOPS = 3 * 2 * D * D * S


def tile_picked_clampprop_none_p_kernel(
    tc, x_words, x_scales, w1, seed, kn, gn, w2, res, w3, offs, e1, e2, mv, out
):
    nc = tc.nc
    with ExitStack() as ctx:
        keep = ctx.enter_context(tc.tile_pool(name="keep", bufs=1))
        psum = ctx.enter_context(tc.psum_pool(name="psum", bufs=1))

        def sb(name, shape, dtype, tag=None):
            return keep.tile(shape, dtype, name=name, tag=tag or name, align_bytes=64)

        def bank(name, shape, number):
            return psum.tile(shape, F32, name=name, tag=f"bank{number}")

        def rows_dealt(dram):
            return dram.rearrange("(p t) c -> p t c", t=PACK)

        def load_list(name, dram):
            tile = keep.tile([P, S // 16], U16, name=name)
            nc.sync.dma_start(tile[:], dram)
            return tile

        def load_rows(name, dram):
            tile = sb(name, [P, PACK, D], F32)
            nc.sync.dma_start(tile[:], rows_dealt(dram))
            return tile

        x_scale_table = sb("x_scale_table", [P, T], U8)
        nc.gpsimd.memset(x_scale_table[:, 0 : T // 2].bitcast(I32), 0)
        nc.vector.memset(x_scale_table[:, T // 2 : T].bitcast(I32), 0)
        offs_sb = load_list("offs_sb", offs)
        gn_sb = sb("gn_sb", [P, PACK], F32)
        nc.sync.dma_start(gn_sb[:], gn.rearrange("(p t) o -> p (t o)", t=PACK))
        w1_raw = load_rows("w1_raw", w1)
        e1_sb = load_list("e1_sb", e1)
        e2_sb = load_list("e2_sb", e2)
        for q in range(4):
            nc.sync.dma_start(
                x_scale_table[32 * q : 32 * q + 4, :].bitcast(I32),
                x_scales[0, 4 * q : 4 * q + 4, :].bitcast(I32),
            )
        x_word_table = sb("x_word_table", [P, T], U32)
        nc.sync.dma_start(
            x_word_table[:].bitcast(I32), x_words[0].rearrange("p n t -> p (n t)").bitcast(I32)
        )
        seed_sb = load_rows("seed_sb", seed)
        w2_raw = load_rows("w2_raw", w2)
        known = sb("known", [P, BLOCKS], F32)
        with nc.allow_non_contiguous_dma(reason="one value of kn a partition and block"):
            nc.sync.dma_start(known[:], kn[0:1, :].rearrange("o (b p) -> p (o b)", p=P))
        mv_sb = load_list("mv_sb", mv)
        w3_raw = load_rows("w3_raw", w3)
        res_sb = load_rows("res_sb", res)

        y = [sb(f"y{t}", [P, 2 * S], F32) for t in range(PACK)]
        for t in range(PACK):
            nc.vector.memset(y[t][:, S : 2 * S], 0.0)
        identity = sb("identity", [P, P], F32)
        make_identity(nc, identity[:])
        widest = MOVE_SLICES[0][1]
        last = PACK - 1
        gain_rows = sb("gain_rows", [P, last, widest], F32)
        nc.vector.tensor_copy(gain_rows[:], gn_sb[:, 0:last].unsqueeze(2).to_broadcast([P, last, widest]))
        gain_last = {}
        for s0, width in MOVE_SLICES:
            gain_last[s0] = sb(f"gain_last{s0}", [P, width], F32)
            nc.vector.tensor_copy(gain_last[s0][:], gn_sb[:, last:PACK].to_broadcast([P, width]))

        def deal_views(grouped, raw, t0, t1):
            dst = grouped[:].rearrange("p (t m j) -> p m j t", m=P, j=PACK)
            src = raw[:].rearrange("p j (m t) -> p m j t", t=PACK)[:, :, :, t0:t1]
            return dst, src

        def quantize(codes, scales, grouped):
            nc.vector.quantize_mx(out=codes.bitcast(FP8X4), scales=scales, in_=grouped)

        def mx_tiles(name, width):
            return sb(name + "_codes", [P, width], U32), sb(name + "_scales", [P, width], U8)

        def quantized(name, grouped, width):
            codes, scales = mx_tiles(name, width)
            quantize(codes[:], scales[:], grouped)
            return codes, scales

        def product(acc, weights, t, moving):
            cols = slice(P * t, P * (t + 1))
            nc.tensor.matmul_mx(
                out=acc,
                lhsT=weights[0][:, cols].bitcast(FP8X4),
                lhsT_scale=weights[1][:, cols],
                rhs=moving[0].bitcast(FP8X4),
                rhs_scale=moving[1],
                start=True,
                stop=True,
            )

        def woven(ap):
            return ap.rearrange("p t (c i) -> p c t i", i=PACK)

        def woven_out(tile):
            return tile[:].rearrange("p (c i t) -> p c t i", i=PACK, t=PACK)

        w1_low = sb("w1_low", [P, 2 * D], BF16, "w1_low")
        w1_high = sb("w1_high", [P, 2 * D], BF16, "w1_high")
        nc.vector.tensor_copy(*deal_views(w1_low, w1_raw, 0, 2))
        nc.scalar.copy(*deal_views(w1_high, w1_raw, 2, 4))
        x_scale_picked = sb("x_scale_picked", [P, S], U8)
        nc.vector.tensor_copy(x_scale_picked[:], x_scale_table[:].indirect(offs_sb[:]))
        w1_q = mx_tiles("w1", D)
        for u, grouped in enumerate((w1_low, w1_high)):
            cols = slice(u * D // 2, (u + 1) * D // 2)
            quantize(w1_q[0][:, cols], w1_q[1][:, cols], grouped[:])

        picked = []
        for h in range(2):
            tile = sb(f"x_word_picked{h}", [P, HALF], U32, ("w1_high", "w1_low")[h])
            nc.vector.tensor_copy(
                tile[:], x_word_table[:].indirect(offs_sb[:, h * HALF // 16 : (h + 1) * HALF // 16])
            )
            picked.append(tile)
        for number, (t, h) in enumerate(((0, 0), (1, 0), (0, 1), (1, 1), (2, 0), (2, 1), (3, 0), (3, 1))):
            cols = slice(h * HALF, (h + 1) * HALF)
            acc = bank(f"y_acc{t}{h}", [P, HALF], number)
            product(acc[:], w1_q, t, (picked[h][:], x_scale_picked[:, cols]))
            if number in (1, 2):
                nc.vector.tensor_scalar(y[t][:, cols], acc[:], gn_sb[:, t : t + 1], None, ALU.mult)
            else:
                nc.scalar.activation(y[t][:, cols], acc[:], ACT.Copy, scale=gn_sb[:, t : t + 1])

        seed_gained = sb("seed_gained", [P, PACK, S], F32)
        for t in range(PACK):
            nc.scalar.activation(seed_gained[:, t, :], seed_sb[:, t, :], ACT.Copy, scale=gn_sb[:, t : t + 1])
        spread = sb("spread", [P, BLOCKS], F32)
        nc.scalar.activation(spread[:], known[:], ACT.Copy, scale=-0.75, bias=0.75)

        def by_feature(turned):
            return turned[:].rearrange("r t p -> r p t")

        held = []
        for b in range(BLOCKS):
            turned = bank(f"seed_turned{b}", [P, PACK, P], b)
            for t in range(PACK):
                nc.tensor.transpose(turned[:, t, :], seed_gained[:, t, P * b : P * (b + 1)], identity[:])
            tile = sb(f"held{b}", [P, P, PACK], F32)
            nc.scalar.activation(tile[:], by_feature(turned), ACT.Copy, scale=known[:, b : b + 1])
            held.append(tile)
        w2_grouped = sb("w2_grouped", [P, PACK * D], BF16)
        nc.scalar.copy(*deal_views(w2_grouped, w2_raw, 0, PACK))
        w3_high = sb("w3_high", [P, 2 * D], BF16)
        nc.scalar.copy(*deal_views(w3_high, w3_raw, 2, 4))

        first = sb("first", [P, PACK, S], F32)
        both = sb("both", [P, PACK, S], F32)
        both_turned = [bank(f"both_turned{b}", [P, PACK, P], b) for b in range(BLOCKS)]
        for step in range(PACK + 1):
            if step < PACK:
                nc.vector.tensor_copy(first[:, step, :], y[step][:].indirect(e1_sb[:]))
            if step >= 1:
                t = step - 1
                nc.vector.tensor_tensor(both[:, t, :], y[t][:].indirect(e2_sb[:]), first[:, t, :], ALU.add)
                for b in range(BLOCKS):
                    nc.tensor.transpose(both_turned[b][:, t, :], both[:, t, P * b : P * (b + 1)], identity[:])
        w2_q = quantized("w2", w2_grouped[:], D)

        z_grouped = {c0: sb(f"z_grouped{c0}", [P, PACK * n], BF16) for c0, n in CHUNKS}
        for b in range(BLOCKS):
            z_turned = sb(f"z_turned{b}", [P, P, PACK], BF16)
            nc.vector.scalar_tensor_tensor(
                z_turned[:], by_feature(both_turned[b]), spread[:, b : b + 1], held[b][:], ALU.mult, ALU.add
            )
            pairs = z_turned[:].rearrange("r p t -> r (p t)").bitcast(F32)
            pairs_back = bank(f"pairs_back{b}", [P, 2, P], BLOCKS + b)
            for u in range(2):
                nc.tensor.transpose(pairs_back[:, u, :], pairs[:, u : 2 * P : 2], identity[:])
            c0 = max(start for start, width in CHUNKS if start <= P * b)
            place = slice(2 * (P * b - c0), 2 * (P * (b + 1) - c0))
            nc.scalar.copy(
                z_grouped[c0][:].bitcast(F32)[:, place].rearrange("p (r u) -> p r u", u=2),
                pairs_back[:].rearrange("p u r -> p r u"),
            )
        z_q = {}
        for c0, n in CHUNKS:
            if c0 + n == S:
                w3_low = sb("w3_low", [P, 2 * D], BF16, f"z_grouped{CHUNKS[-2][0]}")
                nc.vector.tensor_copy(*deal_views(w3_low, w3_raw, 0, 2))
            z_q[c0] = quantized(f"z{c0}", z_grouped[c0][:], n)
        w3_q = (sb("w3_codes", [P, D], U32, f"z_grouped{CHUNKS[-1][0]}"), sb("w3_scales", [P, D], U8))
        for u, grouped in enumerate((w3_low, w3_high)):
            cols = slice(u * D // 2, (u + 1) * D // 2)
            quantize(w3_q[0][:, cols], w3_q[1][:, cols], grouped[:])

        hid = [sb(f"hid{t}", [P, S], F32) for t in range(PACK)]
        wide, narrow = MOVE_SLICES
        for (s0, width), t, number in (
            (wide, 0, 0), (narrow, 0, 4), (wide, 1, 1), (narrow, 1, 5),
            (wide, 2, 4), (narrow, 2, 6), (wide, 3, 5), (narrow, 3, 7),
        ):
            acc = bank(f"h_acc{s0}{t}", [P, width], number)
            for c0, n in CHUNKS:
                if s0 <= c0 < s0 + width:
                    product(acc[:, c0 - s0 : c0 - s0 + n], w2_q, t, (z_q[c0][0][:], z_q[c0][1][:]))
            nc.scalar.activation(hid[t][:, s0 : s0 + width], acc[:], ACT.Tanh)

        out_rows = rows_dealt(out)
        moved = {}
        for c0, n in MOVE_SLICES:
            moved[c0] = sb(f"moved{c0}", [P, PACK, n], F32, "gain_last0" if c0 else None)
            for t in range(PACK):
                nc.vector.tensor_tensor(
                    moved[c0][:, t, :],
                    hid[t][:].indirect(mv_sb[:, c0 // 16 : (c0 + n) // 16]),
                    gain_last[c0][:] if t == last else gain_rows[:, t, 0:n],
                    ALU.mult,
                )
        accs = []
        for c0, n in CHUNKS:
            z2_grouped = sb(f"z2_grouped{c0}", [P, PACK * n], BF16)
            m0 = max(start for start, width in MOVE_SLICES if start <= c0)
            nc.scalar.copy(woven_out(z2_grouped), woven(moved[m0][:, :, c0 - m0 : c0 - m0 + n]))
            z2_q = quantized(f"z2{c0}", z2_grouped[:], n)
            per_bank = 2 if c0 + n == S else S // n
            for t0 in range(0, PACK, per_bank):
                acc = bank(f"o_acc{c0}{t0}", [P, per_bank, n], len(accs))
                for t in range(t0, t0 + per_bank):
                    product(acc[:, t - t0, :], w3_q, t, (z2_q[0][:], z2_q[1][:]))
                accs.append((acc, slice(t0, t0 + per_bank), slice(c0, c0 + n)))
        for b, (acc, ts, cols) in enumerate(accs):
            result = sb(f"result{b}", list(acc.shape), F32)
            nc.vector.tensor_tensor(result[:], acc[:], res_sb[:, ts, cols], ALU.add)
            nc.sync.dma_start(out_rows[:, ts, cols], result[:])
